import numpy as np
import ml_dtypes


def mxq(x, axis, fmt="e4m3"):
    dtype, down = {"e4m3": (ml_dtypes.float8_e4m3fn, 7), "e5m2": (ml_dtypes.float8_e5m2, 14)}[fmt]
    v = np.moveaxis(np.asarray(x, np.float32).astype(ml_dtypes.bfloat16).astype(np.float64), axis, -1)
    blocks = v.reshape(v.shape[:-1] + (-1, 32))
    amax = np.abs(blocks).max(-1, keepdims=True)
    byte = np.maximum(np.where(amax > 0, np.frexp(amax)[1] - 1 + 127, 0) - down, 1)
    scale = np.exp2(byte - 127.0)
    codes = (blocks / scale).astype(np.float32).astype(dtype).astype(np.float64)
    return np.moveaxis((codes * scale).reshape(v.shape), -1, axis)


WIDE = False


def mx_kscale(k):
    if not WIDE:
        return np.ones(k)
    levels = np.array([24, -24, 12, -12, 0])
    if k % 512:
        return np.exp2(np.random.permutation(np.resize(levels, k // 32))).repeat(32)
    a = np.empty((k // 512, 16))
    for p in range(k // 512):
        a[p, :8] = np.random.permutation(np.resize(levels, 8))
        for g in range(8):
            far = levels[np.abs(levels - a[p, g]) >= 10]
            a[p, g + 8] = far[np.random.randint(len(far))]
    return np.exp2(a.ravel()).repeat(32)


def f64(x):
    return np.asarray(x).astype(np.float64)


def striped(idx):
    return np.tile(idx.reshape(-1, 16).T, (8, 1)).astype(np.uint16)


def unstriped(offs):
    return offs[:16].T.reshape(-1).astype(np.int64)


E2M1 = np.array([0.0, 0.5, 1.0, 1.5, 2.0, 3.0, 4.0, 6.0, -0.0, -0.5, -1.0, -1.5, -2.0, -3.0, -4.0, -6.0])


def pack_weight(w, fmt):
    k, n = w.shape
    w = f64(np.asarray(w, np.float32).astype(ml_dtypes.bfloat16)).reshape(k // 32, 32, n)
    amax = np.abs(w).max(1)
    if fmt == "e4m3":
        byte = np.frexp(amax)[1] - 1 + 127 - 7
    else:
        mant, ex = np.frexp(amax / 6.0)
        byte = np.where(mant > 0.5, ex, ex - 1) + 127
    byte = np.clip(np.where(amax > 0, byte, 1), 1, 254)
    scaled = (w * np.exp2(127.0 - byte)[:, None, :]).reshape(k, n).astype(np.float32)
    by_word = np.ascontiguousarray(scaled.reshape(k // 512, 128, 4, n).transpose(0, 1, 3, 2))
    if fmt == "e4m3":
        words = by_word.astype(ml_dtypes.float8_e4m3fn).view(np.uint8)
    else:
        c = by_word.astype(ml_dtypes.float4_e2m1fn).view(np.uint8) & 0xF
        words = (c[..., 0::2] | (c[..., 1::2] << 4)).reshape(k // 512, 128, 2 * n)
    return np.ascontiguousarray(words), np.ascontiguousarray(byte.astype(np.uint8).reshape(k // 512, 16, n))


def unpack_weight(words, scales, fmt):
    g, _, n = scales.shape
    words = np.ascontiguousarray(words).reshape(g, 128, n, -1)
    if fmt == "e4m3":
        vals = words.view(ml_dtypes.float8_e4m3fn).astype(np.float64)
    else:
        nib = np.empty((g, 128, n, 4), np.uint8)
        nib[..., 0::2] = words & 0xF
        nib[..., 1::2] = words >> 4
        vals = E2M1[nib]
    vals = vals * np.repeat(np.exp2(scales.astype(np.float64) - 127.0), 8, axis=1)[..., None]
    return vals.transpose(0, 1, 3, 2).reshape(g * 512, n)


K, R, M, T, N, J = 1024, 1024, 256, 2048, 512, 1024


def setup_inputs():
    n = np.random.standard_normal
    u = mx_kscale(R)[:, None]
    s = mx_kscale(K)[:, None]
    wv = n((R, N)) / np.sqrt(R) / u
    p_w8 = pack_weight(n((K, R)) / np.sqrt(K) / s / u.T, "e4m3")
    p_tab = pack_weight(n((R, T)) * u, "e4m3")
    p_wv4 = pack_weight(wv[512:], "e2m1")
    return {
        "x": (n((K, M)) * s).astype(np.float32),
        "w8_words": p_w8[0],
        "w8_scales": p_w8[1],
        "tab_words": p_tab[0],
        "tab_scales": p_tab[1],
        "wv8": (wv[:512]).astype(np.float32),
        "wv4_words": p_wv4[0],
        "wv4_scales": p_wv4[1],
        "offs": striped(np.random.permutation(T)[:J]),
    }


def reference(x, w8_words, w8_scales, tab_words, tab_scales, wv8, wv4_words, wv4_scales, offs):
    idx = unstriped(offs)
    x_ = mxq(f64(x), 0, "e4m3")
    w8_ = unpack_weight(w8_words, w8_scales, "e4m3")
    qa = w8_.T @ x_
    qa_ = mxq(qa, 0, "e4m3")
    tab_ = unpack_weight(tab_words, tab_scales, "e4m3")[:, idx]
    sc = qa_.T @ tab_
    wv8_ = mxq(f64(wv8), 0, "e4m3")
    wv4_ = unpack_weight(wv4_words, wv4_scales, "e2m1")
    vv = wv8_.T @ tab_[:512] + wv4_.T @ tab_[512:]
    return np.exp(sc * 0.015625), vv

@@ -1,0 +1,248 @@
+from contextlib import ExitStack
+
+import concourse.mybir as mybir
+from concourse.masks import make_identity
+
+K, R, M, T, N, J = 1024, 1024, 256, 2048, 512, 1024
+FLOPS = 2 * K * R * M + 2 * R * M * J + 2 * R * N * J
+
+F32 = mybir.dt.float32
+BF16 = mybir.dt.bfloat16
+I32 = mybir.dt.int32
+U32 = mybir.dt.uint32
+U16 = mybir.dt.uint16
+U8 = mybir.dt.uint8
+FP8X4 = mybir.dt.float8_e4m3fn_x4
+FP4X4 = mybir.dt.float4_e2m1fn_x4
+EXP = mybir.ActivationFunctionType.Exp
+
+P = 128
+PACK = 4
+BANK = 512
+TAB_ROW = (4, 0)
+W8_ROW = (8, 12)
+QA_ROW = (4, 8)
+SCORE_SCALE = 0.015625
+
+
+def interleave(engine_copy, grouped, raw):
+    engine_copy(
+        out=grouped.rearrange("p (c i) t -> p c t i", i=4),
+        in_=raw.rearrange("p t (c i) -> p c t i", i=4),
+    )
+
+
+def tile_list_mlat_qf_exp_kernel(
+    tc, x, w8_words, w8_scales, tab_words, tab_scales, wv8, wv4_words, wv4_scales, offs, out_0, out_1
+):
+    nc = tc.nc
+    with ExitStack() as ctx:
+        sb = ctx.enter_context(tc.tile_pool(name="sb", bufs=1))
+        psum = ctx.enter_context(tc.psum_pool(name="psum", bufs=1))
+
+        def tile(shape, dtype, name, tag=""):
+            return sb.tile(shape, dtype, name=name, tag=tag or name, align_bytes=64)
+
+        banks = [psum.tile([P, BANK], F32, name="bank%d" % b) for b in range(8)]
+        offsets = sb.tile([P, J // 16], U16, name="offsets")
+        tab_s = tile([P, T], U8, "tab_s")
+        w8_s = tile([P, R], U8, "w8_s")
+        wv4_s = tile([P, N], U8, "wv4_s")
+        ident = tile([P, P], F32, "ident")
+        warm = tile([P, 2], F32, "warm")
+        x_raw = tile([P, 2, PACK, M], F32, "x_raw")
+        w8_w = [tile([P, R], I32, "w8_w%d" % a) for a in range(2)]
+        tab_w = [tile([P, T], I32, "tab_w%d" % a) for a in range(2)]
+        wv8_raw = [tile([P, PACK, N // 2], F32, "wv8_raw%d" % h) for h in range(2)]
+        wv4_w = tile([P, 2 * N], U8, "wv4_w")
+
+        nc.vector.memset(w8_s[:].bitcast(I32), 0)
+        nc.gpsimd.memset(tab_s[:].bitcast(I32), 0)
+        nc.vector.memset(warm[:, 0:1], 0.0)
+        nc.vector.memset(wv4_s[:].bitcast(I32), 0)
+        make_identity(nc, ident[:])
+        nc.scalar.activation(out=warm[:, 1:2], in_=warm[:, 0:1], func=EXP)
+
+        def load_w8_scales(q):
+            nc.sync.dma_start(
+                out=w8_s[32 * q + W8_ROW[0] : 32 * q + W8_ROW[0] + 8, :].bitcast(I32),
+                in_=w8_scales[:, 4 * q : 4 * q + 4, :].bitcast(I32),
+            )
+
+        def load_tab_scales(a, r):
+            nc.sync.dma_start(
+                out=tab_s[TAB_ROW[a] + r : P : 32, :].bitcast(I32),
+                in_=tab_scales[a, r:16:4, :].bitcast(I32),
+            )
+
+        def load_tab(a):
+            nc.sync.dma_start(out=tab_w[a][:], in_=tab_words[a].rearrange("p t i -> p (t i)").bitcast(I32))
+
+        def load_w8(a):
+            nc.sync.dma_start(out=w8_w[a][:], in_=w8_words[a].rearrange("p r i -> p (r i)").bitcast(I32))
+
+        tab_rows = [(a, r) for r in range(4) for a in range(2)]
+        nc.sync.dma_start(offsets[:], offs)
+        nc.sync.dma_start(out=x_raw[:], in_=x.rearrange("(a p j) m -> p a j m", a=2, j=PACK))
+        for q in range(4):
+            load_w8_scales(q)
+        for a, r in tab_rows[:2]:
+            load_tab_scales(a, r)
+        load_w8(0)
+        load_w8(1)
+        for a, r in tab_rows[2:]:
+            load_tab_scales(a, r)
+        load_tab(1)
+        for r in range(4):
+            nc.sync.dma_start(out=wv4_s[r:P:32, :].bitcast(I32), in_=wv4_scales[0, r:16:4, :].bitcast(I32))
+        nc.sync.dma_start(out=wv4_w[:].bitcast(I32), in_=wv4_words[0].bitcast(I32))
+        load_tab(0)
+        for h in range(2):
+            nc.sync.dma_start(
+                out=wv8_raw[h][:],
+                in_=wv8.rearrange("(p j) n -> p j n", j=PACK)[:, :, (N // 2) * h : (N // 2) * (h + 1)],
+            )
+
+        def quantise(grouped, name, scales=None):
+            width = grouped.shape[1]
+            codes = tile([P, width], U32, name + "_w")
+            if scales is None:
+                scales = tile([P, width], U8, name + "_s")[:]
+            nc.vector.quantize_mx(
+                out=codes[:].bitcast(FP8X4), scales=scales, in_=grouped[:].rearrange("p w t -> p (w t)")
+            )
+            return codes, scales
+
+        x_b = [tile([P, M, PACK], BF16, "x_b%d" % a) for a in range(2)]
+        interleave(nc.vector.tensor_copy, x_b[0][:], x_raw[:, 0])
+        interleave(nc.scalar.copy, x_b[1][:], x_raw[:, 1])
+        x_q = [quantise(x_b[a], "x_q%d" % a) for a in range(2)]
+
+        def listed(h):
+            return offsets[:, (BANK // 16) * h : (BANK // 16) * (h + 1)]
+
+        got_s = []
+        for h in range(2):
+            g = tile([P, BANK], U8, "got_s%d" % h)
+            nc.vector.tensor_copy(g[:], tab_s[:].indirect(listed(h)))
+            got_s.append(g)
+
+        got_w = {}
+
+        def gather_words(a, h):
+            g = tile([P, BANK], U32, "got_w%d%d" % (a, h))
+            nc.vector.tensor_copy(g[:], tab_w[a][:].bitcast(U32).indirect(listed(h)))
+            got_w[(a, h)] = g
+
+        qa_q = {}
+
+        def query_pass(bank, a, h, mt):
+            nc.tensor.matmul_mx(
+                out=bank[:],
+                lhsT=x_q[a][0][:, P * mt : P * (mt + 1)].bitcast(FP8X4),
+                lhsT_scale=x_q[a][1][:, P * mt : P * (mt + 1)],
+                rhs=w8_w[a][:, BANK * h : BANK * (h + 1)].bitcast(FP8X4),
+                rhs_scale=w8_s[W8_ROW[a] : P, BANK * h : BANK * (h + 1)],
+                start=(a == 0),
+                stop=(a == 1),
+            )
+
+        def turn_queries(h, sum_banks, turn_bank):
+            rows = []
+            for mt in range(2):
+                row = tile([P, 2, P, 2], BF16, "qa_row%d%d" % (h, mt))
+                nc.scalar.copy(out=row[:], in_=sum_banks[mt][:].rearrange("m (p u e) -> m u p e", u=2, e=2))
+                rows.append(row)
+            for mt in range(2):
+                words = rows[mt][:].rearrange("m u p e -> m (u p e)").bitcast(F32)
+                for u in range(2):
+                    col = P * (2 * mt + u)
+                    nc.tensor.transpose(turn_bank[:, col : col + P], words[:, P * u : P * (u + 1)], ident[:])
+            grouped = tile([P, M, PACK], BF16, "qa_b%d" % h)
+            nc.scalar.copy(
+                out=grouped[:].bitcast(F32).rearrange("p (t m) u -> p t m u", t=2),
+                in_=turn_bank[:].rearrange("p (t u m) -> p t m u", t=2, u=2),
+            )
+            return grouped
+
+        def score_pass(bank, a, mt, h):
+            nc.tensor.matmul_mx(
+                out=bank[:],
+                lhsT=qa_q[a][0][:, P * mt : P * (mt + 1)].bitcast(FP8X4),
+                lhsT_scale=qa_q[a][1][:, P * mt : P * (mt + 1)],
+                rhs=got_w[(a, h)][:].bitcast(FP8X4),
+                rhs_scale=got_s[h][TAB_ROW[a] : P, :],
+                start=(a == 1),
+                stop=(a == 0),
+            )
+
+        wv8_q = {}
+
+        def value_pass(bank, a, nt, h, first):
+            if a == 1:
+                lhsT = wv4_w[:, 2 * P * nt : 2 * P * (nt + 1)].bitcast(FP4X4)
+                lhsT_scale = wv4_s[:, P * nt : P * (nt + 1)]
+            else:
+                codes, scales = wv8_q[nt // 2]
+                lhsT = codes[:, P * (nt % 2) : P * (nt % 2 + 1)].bitcast(FP8X4)
+                lhsT_scale = scales[:, P * (nt % 2) : P * (nt % 2 + 1)]
+            nc.tensor.matmul_mx(
+                out=bank[:],
+                lhsT=lhsT,
+                lhsT_scale=lhsT_scale,
+                rhs=got_w[(a, h)][:].bitcast(FP8X4),
+                rhs_scale=got_s[h][TAB_ROW[a] : P, :],
+                start=first,
+                stop=not first,
+            )
+
+        def finish_scores(bank, mt, h, res):
+            score_pass(bank, 0, mt, h)
+            nc.scalar.activation(out=res[:], in_=bank[:], func=EXP, scale=SCORE_SCALE)
+            nc.sync.dma_start(out=out_0[P * mt : P * (mt + 1), BANK * h : BANK * (h + 1)], in_=res[:])
+
+        def finish_values(bank, a, nt, h, engine_copy):
+            value_pass(bank, a, nt, h, False)
+            res = tile([P, BANK], F32, "val%d%d" % (nt, h))
+            engine_copy(out=res[:], in_=bank[:])
+            nc.sync.dma_start(out=out_1[P * nt : P * (nt + 1), BANK * h : BANK * (h + 1)], in_=res[:])
+
+        def quantise_wv8(h, engine_copy):
+            grouped = tile([P, N // 2, PACK], BF16, "wv8_b%d" % h)
+            interleave(engine_copy, grouped[:], wv8_raw[h][:])
+            wv8_q[h] = quantise(grouped, "wv8_q%d" % h)
+
+        for a in range(2):
+            for b, (h, mt) in enumerate(((1, 0), (1, 1), (0, 0), (0, 1))):
+                query_pass(banks[b], a, h, mt)
+        qa_b1 = turn_queries(1, banks[0:2], banks[4])
+        qa_b0 = turn_queries(0, banks[2:4], banks[5])
+        gather_words(1, 0)
+        gather_words(1, 1)
+        for nt in range(4):
+            value_pass(banks[nt], 1, nt, 0, True)
+        qa_q[1] = quantise(qa_b1, "qa_q1", wv4_s[QA_ROW[1] : P, 0:M])
+        qa_q[0] = quantise(qa_b0, "qa_q0", wv4_s[QA_ROW[0] : P, 0:M])
+        for mt in range(2):
+            score_pass(banks[6 + mt], 1, mt, 0)
+        for mt in range(2):
+            score_pass(banks[4 + mt], 1, mt, 1)
+        gather_words(0, 0)
+        gather_words(0, 1)
+        quantise_wv8(0, nc.scalar.copy)
+        exps = tile([P, 4 * BANK], F32, "exps", "wv8_raw0")
+        for h in range(2):
+            for mt in range(2):
+                c = BANK * (2 * h + mt)
+                finish_scores(banks[6 - 2 * h + mt], mt, h, exps[:, c : c + BANK])
+        quantise_wv8(1, nc.vector.tensor_copy)
+        finish_values(banks[0], 0, 0, 0, nc.vector.tensor_copy)
+        finish_values(banks[1], 0, 1, 0, nc.scalar.copy)
+        for nt in range(2):
+            value_pass(banks[6 + nt], 1, nt, 1, True)
+            finish_values(banks[6 + nt], 0, nt, 1, nc.scalar.copy if nt % 2 else nc.vector.tensor_copy)
+        for nt in range(2, 4):
+            finish_values(banks[nt], 0, nt, 0, nc.scalar.copy if nt % 2 else nc.vector.tensor_copy)
+        for nt in range(2, 4):
+            value_pass(banks[2 + nt], 1, nt, 1, True)
+            finish_values(banks[2 + nt], 0, nt, 1, nc.scalar.copy if nt % 2 else nc.vector.tensor_copy)

@@ -50,7 +50,7 @@ def tile_list_mlat_qf_exp_kernel(
         wv4_s = tile([P, N], U8, "wv4_s")
         ident = tile([P, P], F32, "ident")
         warm = tile([P, 2], F32, "warm")
-        x_raw = tile([P, 2, PACK, M], F32, "x_raw")
+        x_raw = [tile([P, PACK, M], F32, "x_raw%d" % a) for a in range(2)]
         w8_w = [tile([P, R], I32, "w8_w%d" % a) for a in range(2)]
         tab_w = [tile([P, T], I32, "tab_w%d" % a) for a in range(2)]
         wv8_raw = [tile([P, PACK, N // 2], F32, "wv8_raw%d" % h) for h in range(2)]
@@ -60,7 +60,6 @@ def tile_list_mlat_qf_exp_kernel(
         nc.gpsimd.memset(tab_s[:].bitcast(I32), 0)
         nc.vector.memset(warm[:, 0:1], 0.0)
         nc.vector.memset(wv4_s[:].bitcast(I32), 0)
-        make_identity(nc, ident[:])
         nc.scalar.activation(out=warm[:, 1:2], in_=warm[:, 0:1], func=EXP)
 
         def load_w8_scales(q):
@@ -69,8 +68,13 @@ def tile_list_mlat_qf_exp_kernel(
                 in_=w8_scales[:, 4 * q : 4 * q + 4, :].bitcast(I32),
             )
 
-        def load_tab_scales(a, r):
+        def load_x(a):
             nc.sync.dma_start(
+                out=x_raw[a][:], in_=x[512 * a : 512 * (a + 1), :].rearrange("(p j) m -> p j m", j=PACK)
+            )
+
+        def load_tab_scales(queue, a, r):
+            queue.dma_start(
                 out=tab_s[TAB_ROW[a] + r : P : 32, :].bitcast(I32),
                 in_=tab_scales[a, r:16:4, :].bitcast(I32),
             )
@@ -83,15 +87,16 @@ def tile_list_mlat_qf_exp_kernel(
 
         tab_rows = [(a, r) for r in range(4) for a in range(2)]
         nc.sync.dma_start(offsets[:], offs)
-        nc.sync.dma_start(out=x_raw[:], in_=x.rearrange("(a p j) m -> p a j m", a=2, j=PACK))
+        load_x(0)
+        load_w8(0)
         for q in range(4):
             load_w8_scales(q)
-        for a, r in tab_rows[:2]:
-            load_tab_scales(a, r)
-        load_w8(0)
+        load_x(1)
         load_w8(1)
-        for a, r in tab_rows[2:]:
-            load_tab_scales(a, r)
+        for r in range(4):
+            load_tab_scales(nc.sync, 1, r)
+            load_tab_scales(nc.gpsimd, 0, r)
+        make_identity(nc, ident[:])
         load_tab(1)
         for r in range(4):
             nc.sync.dma_start(out=wv4_s[r:P:32, :].bitcast(I32), in_=wv4_scales[0, r:16:4, :].bitcast(I32))
@@ -114,9 +119,10 @@ def tile_list_mlat_qf_exp_kernel(
             return codes, scales
 
         x_b = [tile([P, M, PACK], BF16, "x_b%d" % a) for a in range(2)]
-        interleave(nc.vector.tensor_copy, x_b[0][:], x_raw[:, 0])
-        interleave(nc.scalar.copy, x_b[1][:], x_raw[:, 1])
-        x_q = [quantise(x_b[a], "x_q%d" % a) for a in range(2)]
+        x_q = []
+        for a in range(2):
+            interleave(nc.vector.tensor_copy, x_b[a][:], x_raw[a][:])
+            x_q.append(quantise(x_b[a], "x_q%d" % a))
 
         def listed(h):
             return offsets[:, (BANK // 16) * h : (BANK // 16) * (h + 1)]

@@ -21,7 +21,6 @@ PACK = 4
 BANK = 512
 TAB_ROW = (4, 0)
 W8_ROW = (8, 12)
-QA_ROW = (4, 8)
 SCORE_SCALE = 0.015625
 
 
@@ -48,30 +47,18 @@ def tile_list_mlat_qf_exp_kernel(
         tab_s = tile([P, T], U8, "tab_s")
         w8_s = tile([P, R], U8, "w8_s")
         wv4_s = tile([P, N], U8, "wv4_s")
-        ident = tile([P, P], F32, "ident")
         warm = tile([P, 2], F32, "warm")
         x_raw = [tile([P, PACK, M], F32, "x_raw%d" % a) for a in range(2)]
-        w8_w = [tile([P, R], I32, "w8_w%d" % a) for a in range(2)]
+        w8_w = [tile([P, 2, BANK], I32, "w8_w%d" % h) for h in range(2)]
         tab_w = [tile([P, T], I32, "tab_w%d" % a) for a in range(2)]
-        wv8_raw = [tile([P, PACK, N // 2], F32, "wv8_raw%d" % h) for h in range(2)]
+        wv8_raw = tile([P, PACK, N], F32, "wv8_raw")
         wv4_w = tile([P, 2 * N], U8, "wv4_w")
 
-        nc.vector.memset(w8_s[:].bitcast(I32), 0)
         nc.gpsimd.memset(tab_s[:].bitcast(I32), 0)
         nc.vector.memset(warm[:, 0:1], 0.0)
         nc.vector.memset(wv4_s[:].bitcast(I32), 0)
+        nc.vector.memset(w8_s[:].bitcast(I32), 0)
         nc.scalar.activation(out=warm[:, 1:2], in_=warm[:, 0:1], func=EXP)
-
-        def load_w8_scales(q):
-            nc.sync.dma_start(
-                out=w8_s[32 * q + W8_ROW[0] : 32 * q + W8_ROW[0] + 8, :].bitcast(I32),
-                in_=w8_scales[:, 4 * q : 4 * q + 4, :].bitcast(I32),
-            )
-
-        def load_x(a):
-            nc.sync.dma_start(
-                out=x_raw[a][:], in_=x[512 * a : 512 * (a + 1), :].rearrange("(p j) m -> p j m", j=PACK)
-            )
 
         def load_tab_scales(queue, a, r):
             queue.dma_start(
@@ -82,109 +69,68 @@ def tile_list_mlat_qf_exp_kernel(
         def load_tab(a):
             nc.sync.dma_start(out=tab_w[a][:], in_=tab_words[a].rearrange("p t i -> p (t i)").bitcast(I32))
 
-        def load_w8(a):
-            nc.sync.dma_start(out=w8_w[a][:], in_=w8_words[a].rearrange("p r i -> p (r i)").bitcast(I32))
-
         tab_rows = [(a, r) for r in range(4) for a in range(2)]
         nc.sync.dma_start(offsets[:], offs)
-        load_x(0)
-        load_w8(0)
-        for q in range(4):
-            load_w8_scales(q)
-        load_x(1)
-        load_w8(1)
-        for r in range(4):
-            load_tab_scales(nc.sync, 1, r)
-            load_tab_scales(nc.gpsimd, 0, r)
-        make_identity(nc, ident[:])
         load_tab(1)
+        for a, r in tab_rows[:6]:
+            load_tab_scales(nc.sync, a, r)
+        for a, r in tab_rows[6:]:
+            load_tab_scales(nc.gpsimd, a, r)
+        ident = tile([P, P], F32, "ident")
+        make_identity(nc, ident[:])
+        nc.sync.dma_start(out=wv8_raw[:], in_=wv8.rearrange("(p j) n -> p j n", j=PACK))
+        nc.sync.dma_start(out=wv4_w[:].bitcast(I32), in_=wv4_words[0].bitcast(I32))
         for r in range(4):
             nc.sync.dma_start(out=wv4_s[r:P:32, :].bitcast(I32), in_=wv4_scales[0, r:16:4, :].bitcast(I32))
-        nc.sync.dma_start(out=wv4_w[:].bitcast(I32), in_=wv4_words[0].bitcast(I32))
         load_tab(0)
-        for h in range(2):
+        for a in range(2):
             nc.sync.dma_start(
-                out=wv8_raw[h][:],
-                in_=wv8.rearrange("(p j) n -> p j n", j=PACK)[:, :, (N // 2) * h : (N // 2) * (h + 1)],
+                out=x_raw[a][:], in_=x[512 * a : 512 * (a + 1), :].rearrange("(p j) m -> p j m", j=PACK)
+            )
+        for q in range(4):
+            nc.sync.dma_start(
+                out=w8_s[32 * q + W8_ROW[0] : 32 * q + W8_ROW[0] + 8, :].bitcast(I32),
+                in_=w8_scales[:, 4 * q : 4 * q + 4, :].bitcast(I32),
+            )
+        for h in (1, 0):
+            nc.sync.dma_start(
+                out=w8_w[h][:],
+                in_=w8_words.rearrange("a p r i -> p a (r i)")[:, :, 4 * BANK * h : 4 * BANK * (h + 1)].bitcast(I32),
             )
 
-        def quantise(grouped, name, scales=None):
+        def quantise(grouped, name, tag=""):
             width = grouped.shape[1]
-            codes = tile([P, width], U32, name + "_w")
-            if scales is None:
-                scales = tile([P, width], U8, name + "_s")[:]
+            codes = tile([P, width], U32, name + "_w", tag)
+            scales = tile([P, width], U8, name + "_s")
             nc.vector.quantize_mx(
-                out=codes[:].bitcast(FP8X4), scales=scales, in_=grouped[:].rearrange("p w t -> p (w t)")
+                out=codes[:].bitcast(FP8X4), scales=scales[:], in_=grouped[:].rearrange("p w t -> p (w t)")
             )
             return codes, scales
-
-        x_b = [tile([P, M, PACK], BF16, "x_b%d" % a) for a in range(2)]
-        x_q = []
-        for a in range(2):
-            interleave(nc.vector.tensor_copy, x_b[a][:], x_raw[a][:])
-            x_q.append(quantise(x_b[a], "x_q%d" % a))
 
         def listed(h):
             return offsets[:, (BANK // 16) * h : (BANK // 16) * (h + 1)]
 
-        got_s = []
-        for h in range(2):
+        got_s = {}
+        got_w = {}
+
+        def gather_scales(h):
             g = tile([P, BANK], U8, "got_s%d" % h)
             nc.vector.tensor_copy(g[:], tab_s[:].indirect(listed(h)))
-            got_s.append(g)
-
-        got_w = {}
+            got_s[h] = g
 
         def gather_words(a, h):
             g = tile([P, BANK], U32, "got_w%d%d" % (a, h))
             nc.vector.tensor_copy(g[:], tab_w[a][:].bitcast(U32).indirect(listed(h)))
             got_w[(a, h)] = g
 
-        qa_q = {}
-
-        def query_pass(bank, a, h, mt):
-            nc.tensor.matmul_mx(
-                out=bank[:],
-                lhsT=x_q[a][0][:, P * mt : P * (mt + 1)].bitcast(FP8X4),
-                lhsT_scale=x_q[a][1][:, P * mt : P * (mt + 1)],
-                rhs=w8_w[a][:, BANK * h : BANK * (h + 1)].bitcast(FP8X4),
-                rhs_scale=w8_s[W8_ROW[a] : P, BANK * h : BANK * (h + 1)],
-                start=(a == 0),
-                stop=(a == 1),
-            )
-
-        def turn_queries(h, sum_banks, turn_bank):
-            rows = []
-            for mt in range(2):
-                row = tile([P, 2, P, 2], BF16, "qa_row%d%d" % (h, mt))
-                nc.scalar.copy(out=row[:], in_=sum_banks[mt][:].rearrange("m (p u e) -> m u p e", u=2, e=2))
-                rows.append(row)
-            for mt in range(2):
-                words = rows[mt][:].rearrange("m u p e -> m (u p e)").bitcast(F32)
-                for u in range(2):
-                    col = P * (2 * mt + u)
-                    nc.tensor.transpose(turn_bank[:, col : col + P], words[:, P * u : P * (u + 1)], ident[:])
-            grouped = tile([P, M, PACK], BF16, "qa_b%d" % h)
-            nc.scalar.copy(
-                out=grouped[:].bitcast(F32).rearrange("p (t m) u -> p t m u", t=2),
-                in_=turn_bank[:].rearrange("p (t u m) -> p t m u", t=2, u=2),
-            )
-            return grouped
-
-        def score_pass(bank, a, mt, h):
-            nc.tensor.matmul_mx(
-                out=bank[:],
-                lhsT=qa_q[a][0][:, P * mt : P * (mt + 1)].bitcast(FP8X4),
-                lhsT_scale=qa_q[a][1][:, P * mt : P * (mt + 1)],
-                rhs=got_w[(a, h)][:].bitcast(FP8X4),
-                rhs_scale=got_s[h][TAB_ROW[a] : P, :],
-                start=(a == 1),
-                stop=(a == 0),
-            )
-
         wv8_q = {}
 
-        def value_pass(bank, a, nt, h, first):
+        def quantise_wv8(c):
+            grouped = tile([P, N // 2, PACK], BF16, "wv8_b%d" % c)
+            interleave(nc.scalar.copy, grouped[:], wv8_raw[:, :, (N // 2) * c : (N // 2) * (c + 1)])
+            wv8_q[c] = quantise(grouped, "wv8_q%d" % c, "tab_s" if c == 0 else "")
+
+        def value_pass(a, nt, h):
             if a == 1:
                 lhsT = wv4_w[:, 2 * P * nt : 2 * P * (nt + 1)].bitcast(FP4X4)
                 lhsT_scale = wv4_s[:, P * nt : P * (nt + 1)]
@@ -193,62 +139,104 @@ def tile_list_mlat_qf_exp_kernel(
                 lhsT = codes[:, P * (nt % 2) : P * (nt % 2 + 1)].bitcast(FP8X4)
                 lhsT_scale = scales[:, P * (nt % 2) : P * (nt % 2 + 1)]
             nc.tensor.matmul_mx(
-                out=bank[:],
+                out=banks[4 * h + nt][:],
                 lhsT=lhsT,
                 lhsT_scale=lhsT_scale,
                 rhs=got_w[(a, h)][:].bitcast(FP8X4),
                 rhs_scale=got_s[h][TAB_ROW[a] : P, :],
-                start=first,
-                stop=not first,
+                start=(a == 1),
+                stop=(a == 0),
             )
 
-        def finish_scores(bank, mt, h, res):
-            score_pass(bank, 0, mt, h)
-            nc.scalar.activation(out=res[:], in_=bank[:], func=EXP, scale=SCORE_SCALE)
-            nc.sync.dma_start(out=out_0[P * mt : P * (mt + 1), BANK * h : BANK * (h + 1)], in_=res[:])
-
-        def finish_values(bank, a, nt, h, engine_copy):
-            value_pass(bank, a, nt, h, False)
-            res = tile([P, BANK], F32, "val%d%d" % (nt, h))
-            engine_copy(out=res[:], in_=bank[:])
-            nc.sync.dma_start(out=out_1[P * nt : P * (nt + 1), BANK * h : BANK * (h + 1)], in_=res[:])
-
-        def quantise_wv8(h, engine_copy):
-            grouped = tile([P, N // 2, PACK], BF16, "wv8_b%d" % h)
-            interleave(engine_copy, grouped[:], wv8_raw[h][:])
-            wv8_q[h] = quantise(grouped, "wv8_q%d" % h)
-
-        for a in range(2):
-            for b, (h, mt) in enumerate(((1, 0), (1, 1), (0, 0), (0, 1))):
-                query_pass(banks[b], a, h, mt)
-        qa_b1 = turn_queries(1, banks[0:2], banks[4])
-        qa_b0 = turn_queries(0, banks[2:4], banks[5])
-        gather_words(1, 0)
-        gather_words(1, 1)
-        for nt in range(4):
-            value_pass(banks[nt], 1, nt, 0, True)
-        qa_q[1] = quantise(qa_b1, "qa_q1", wv4_s[QA_ROW[1] : P, 0:M])
-        qa_q[0] = quantise(qa_b0, "qa_q0", wv4_s[QA_ROW[0] : P, 0:M])
-        for mt in range(2):
-            score_pass(banks[6 + mt], 1, mt, 0)
-        for mt in range(2):
-            score_pass(banks[4 + mt], 1, mt, 1)
-        gather_words(0, 0)
-        gather_words(0, 1)
-        quantise_wv8(0, nc.scalar.copy)
-        exps = tile([P, 4 * BANK], F32, "exps", "wv8_raw0")
         for h in range(2):
+            gather_words(1, h)
+        for h in range(2):
+            gather_scales(h)
+        for c in range(2):
+            quantise_wv8(c)
+        for h in range(2):
+            gather_words(0, h)
+        for a in (1, 0):
+            for h in range(2):
+                for nt in range(4):
+                    value_pass(a, nt, h)
+
+        x_q = []
+        for a in range(2):
+            grouped = tile([P, M, PACK], BF16, "x_b%d" % a)
+            interleave(nc.scalar.copy, grouped[:], x_raw[a][:])
+            x_q.append(quantise(grouped, "x_q%d" % a))
+
+        values = tile([P, 4, J], F32, "values", "x_raw1")
+
+        def finish_values(nt):
+            nc.scalar.copy(out=values[:, nt, 0:BANK], in_=banks[nt][:])
+            nc.vector.tensor_copy(out=values[:, nt, BANK:J], in_=banks[4 + nt][:])
+            nc.sync.dma_start(out=out_1[P * nt : P * (nt + 1), :], in_=values[:, nt, :])
+
+        rows = {}
+
+        def project_queries(h, sum_banks):
             for mt in range(2):
-                c = BANK * (2 * h + mt)
-                finish_scores(banks[6 - 2 * h + mt], mt, h, exps[:, c : c + BANK])
-        quantise_wv8(1, nc.vector.tensor_copy)
-        finish_values(banks[0], 0, 0, 0, nc.vector.tensor_copy)
-        finish_values(banks[1], 0, 1, 0, nc.scalar.copy)
-        for nt in range(2):
-            value_pass(banks[6 + nt], 1, nt, 1, True)
-            finish_values(banks[6 + nt], 0, nt, 1, nc.scalar.copy if nt % 2 else nc.vector.tensor_copy)
-        for nt in range(2, 4):
-            finish_values(banks[nt], 0, nt, 0, nc.scalar.copy if nt % 2 else nc.vector.tensor_copy)
-        for nt in range(2, 4):
-            value_pass(banks[2 + nt], 1, nt, 1, True)
-            finish_values(banks[2 + nt], 0, nt, 1, nc.scalar.copy if nt % 2 else nc.vector.tensor_copy)
+                for a in range(2):
+                    nc.tensor.matmul_mx(
+                        out=sum_banks[mt][:],
+                        lhsT=x_q[a][0][:, P * mt : P * (mt + 1)].bitcast(FP8X4),
+                        lhsT_scale=x_q[a][1][:, P * mt : P * (mt + 1)],
+                        rhs=w8_w[h][:, a, :].bitcast(FP8X4),
+                        rhs_scale=w8_s[W8_ROW[a] : P, BANK * h : BANK * (h + 1)],
+                        start=(a == 0),
+                        stop=(a == 1),
+                    )
+
+        def round_queries(h, sum_banks):
+            for mt, engine_copy in enumerate((nc.scalar.copy, nc.vector.tensor_copy)):
+                row = tile([P, 2, P, 2], BF16, "qa_row%d%d" % (h, mt))
+                engine_copy(out=row[:], in_=sum_banks[mt][:].rearrange("m (p u e) -> m u p e", u=2, e=2))
+                rows[(h, mt)] = row
+
+        def turn_queries(mt, turn_bank):
+            for h in (1, 0):
+                words = rows[(h, mt)][:].rearrange("m u p e -> m (u p e)").bitcast(F32)
+                for u in range(2):
+                    col = P * (2 * h + u)
+                    nc.tensor.transpose(turn_bank[:, col : col + P], words[:, P * u : P * (u + 1)], ident[:])
+            grouped = tile([P, 2 * P, PACK], BF16, "qa_b%d" % mt)
+            nc.scalar.copy(
+                out=grouped[:].bitcast(F32).rearrange("p (h m) u -> p h m u", h=2),
+                in_=turn_bank[:].rearrange("p (h u m) -> p h m u", h=2, u=2),
+            )
+            return quantise(grouped, "qa_q%d" % mt)
+
+        def finish_scores(mt, qa_q, score_banks):
+            codes, scales = qa_q
+            for h in range(2):
+                for a in range(2):
+                    nc.tensor.matmul_mx(
+                        out=score_banks[h][:],
+                        lhsT=codes[:, P * a : P * (a + 1)].bitcast(FP8X4),
+                        lhsT_scale=scales[:, P * a : P * (a + 1)],
+                        rhs=got_w[(a, h)][:].bitcast(FP8X4),
+                        rhs_scale=got_s[h][TAB_ROW[a] : P, :],
+                        start=(a == 0),
+                        stop=(a == 1),
+                    )
+                res = tile([P, BANK], F32, "exp%d%d" % (mt, h))
+                nc.scalar.activation(out=res[:], in_=score_banks[h][:], func=EXP, scale=SCORE_SCALE)
+                nc.sync.dma_start(out=out_0[P * mt : P * (mt + 1), BANK * h : BANK * (h + 1)], in_=res[:])
+
+        finish_values(0)
+        finish_values(1)
+        project_queries(1, banks[0:2])
+        round_queries(1, banks[0:2])
+        project_queries(0, banks[4:6])
+        round_queries(0, banks[4:6])
+        finish_values(2)
+        nc.vector.tensor_copy(out=values[:, 3, 0:BANK], in_=banks[7][:])
+        nc.sync.dma_start(out=out_1[3 * P : 4 * P, BANK:J], in_=values[:, 3, 0:BANK])
+        qa_q = [turn_queries(0, banks[2]), turn_queries(1, banks[6])]
+        last = tile([P, BANK], F32, "last", "qa_row00")
+        nc.vector.tensor_copy(out=last[:], in_=banks[3][:])
+        nc.sync.dma_start(out=out_1[3 * P : 4 * P, 0:BANK], in_=last[:])
+        finish_scores(0, qa_q[0], banks[0:2])
+        finish_scores(1, qa_q[1], banks[4:6])

@@ -20,7 +20,7 @@ P = 128
 PACK = 4
 BANK = 512
 TAB_ROW = (4, 0)
-W8_ROW = (8, 12)
+W8_ROW = 8
 SCORE_SCALE = 0.015625
 
 
@@ -45,7 +45,7 @@ def tile_list_mlat_qf_exp_kernel(
         banks = [psum.tile([P, BANK], F32, name="bank%d" % b) for b in range(8)]
         offsets = sb.tile([P, J // 16], U16, name="offsets")
         tab_s = tile([P, T], U8, "tab_s")
-        w8_s = tile([P, R], U8, "w8_s")
+        w8_s = tile([P, 2, R], U8, "w8_s")
         wv4_s = tile([P, N], U8, "wv4_s")
         warm = tile([P, 2], F32, "warm")
         x_raw = [tile([P, PACK, M], F32, "x_raw%d" % a) for a in range(2)]
@@ -87,10 +87,10 @@ def tile_list_mlat_qf_exp_kernel(
             nc.sync.dma_start(
                 out=x_raw[a][:], in_=x[512 * a : 512 * (a + 1), :].rearrange("(p j) m -> p j m", j=PACK)
             )
-        for q in range(4):
+        for r in range(4):
             nc.sync.dma_start(
-                out=w8_s[32 * q + W8_ROW[0] : 32 * q + W8_ROW[0] + 8, :].bitcast(I32),
-                in_=w8_scales[:, 4 * q : 4 * q + 4, :].bitcast(I32),
+                out=w8_s[W8_ROW + r : P : 32, :, :].bitcast(I32),
+                in_=w8_scales[:, r:16:4, :].rearrange("a q c -> q a c").bitcast(I32),
             )
         for h in (1, 0):
             nc.sync.dma_start(
@@ -150,6 +150,16 @@ def tile_list_mlat_qf_exp_kernel(
 
         for h in range(2):
             gather_words(1, h)
+        for nt in range(3):
+            nc.tensor.matmul_mx(
+                out=banks[7][:],
+                lhsT=wv4_w[:, 2 * P * nt : 2 * P * (nt + 1)].bitcast(FP4X4),
+                lhsT_scale=wv4_s[:, P * nt : P * (nt + 1)],
+                rhs=got_w[(1, 0)][:].bitcast(FP8X4),
+                rhs_scale=wv4_s[:],
+                start=True,
+                stop=True,
+            )
         for h in range(2):
             gather_scales(h)
         for c in range(2):
@@ -184,7 +194,7 @@ def tile_list_mlat_qf_exp_kernel(
                         lhsT=x_q[a][0][:, P * mt : P * (mt + 1)].bitcast(FP8X4),
                         lhsT_scale=x_q[a][1][:, P * mt : P * (mt + 1)],
                         rhs=w8_w[h][:, a, :].bitcast(FP8X4),
-                        rhs_scale=w8_s[W8_ROW[a] : P, BANK * h : BANK * (h + 1)],
+                        rhs_scale=w8_s[W8_ROW:P, a, BANK * h : BANK * (h + 1)],
                         start=(a == 0),
                         stop=(a == 1),
                     )
@@ -195,17 +205,27 @@ def tile_list_mlat_qf_exp_kernel(
                 engine_copy(out=row[:], in_=sum_banks[mt][:].rearrange("m (p u e) -> m u p e", u=2, e=2))
                 rows[(h, mt)] = row
 
-        def turn_queries(mt, turn_bank):
-            for h in (1, 0):
-                words = rows[(h, mt)][:].rearrange("m u p e -> m (u p e)").bitcast(F32)
-                for u in range(2):
-                    col = P * (2 * h + u)
-                    nc.tensor.transpose(turn_bank[:, col : col + P], words[:, P * u : P * (u + 1)], ident[:])
+        def turn_half(h, mt, turn_bank):
+            words = rows[(h, mt)][:].rearrange("m u p e -> m (u p e)").bitcast(F32)
+            for u in range(2):
+                col = P * (2 * h + u)
+                nc.tensor.transpose(turn_bank[:, col : col + P], words[:, P * u : P * (u + 1)], ident[:])
+
+        def turn_queries(mt, turn_banks):
             grouped = tile([P, 2 * P, PACK], BF16, "qa_b%d" % mt)
-            nc.scalar.copy(
-                out=grouped[:].bitcast(F32).rearrange("p (h m) u -> p h m u", h=2),
-                in_=turn_bank[:].rearrange("p (h u m) -> p h m u", h=2, u=2),
-            )
+            for h in (1, 0):
+                turn_half(h, mt, banks[turn_banks[h]])
+            if len(set(turn_banks)) == 1:
+                nc.scalar.copy(
+                    out=grouped[:].bitcast(F32).rearrange("p (h m) u -> p h m u", h=2),
+                    in_=banks[turn_banks[0]][:].rearrange("p (h u m) -> p h m u", h=2, u=2),
+                )
+            else:
+                for h in (1, 0):
+                    nc.scalar.copy(
+                        out=grouped[:, P * h : P * (h + 1), :].bitcast(F32),
+                        in_=banks[turn_banks[h]][:, 2 * P * h : 2 * P * (h + 1)].rearrange("p (u m) -> p m u", u=2),
+                    )
             return quantise(grouped, "qa_q%d" % mt)
 
         def finish_scores(mt, qa_q, score_banks):
@@ -234,7 +254,7 @@ def tile_list_mlat_qf_exp_kernel(
         finish_values(2)
         nc.vector.tensor_copy(out=values[:, 3, 0:BANK], in_=banks[7][:])
         nc.sync.dma_start(out=out_1[3 * P : 4 * P, BANK:J], in_=values[:, 3, 0:BANK])
-        qa_q = [turn_queries(0, banks[2]), turn_queries(1, banks[6])]
+        qa_q = [turn_queries(0, (6, 2)), turn_queries(1, (7, 7))]
         last = tile([P, BANK], F32, "last", "qa_row00")
         nc.vector.tensor_copy(out=last[:], in_=banks[3][:])
         nc.sync.dma_start(out=out_1[3 * P : 4 * P, 0:BANK], in_=last[:])

@@ -49,14 +49,14 @@ def tile_list_mlat_qf_exp_kernel(
         wv4_s = tile([P, N], U8, "wv4_s")
         warm = tile([P, 2], F32, "warm")
         x_raw = [tile([P, PACK, M], F32, "x_raw%d" % a) for a in range(2)]
-        w8_w = [tile([P, 2, BANK], I32, "w8_w%d" % h) for h in range(2)]
+        w8_w = tile([P, 2, R], I32, "w8_w")
         tab_w = [tile([P, T], I32, "tab_w%d" % a) for a in range(2)]
-        wv8_raw = tile([P, PACK, N], F32, "wv8_raw")
+        wv8_raw = [tile([P, PACK, N // 2], F32, "wv8_raw%d" % c) for c in range(2)]
         wv4_w = tile([P, 2 * N], U8, "wv4_w")
 
         nc.gpsimd.memset(tab_s[:].bitcast(I32), 0)
+        nc.gpsimd.memset(wv4_s[:].bitcast(I32), 0)
         nc.vector.memset(warm[:, 0:1], 0.0)
-        nc.vector.memset(wv4_s[:].bitcast(I32), 0)
         nc.vector.memset(w8_s[:].bitcast(I32), 0)
         nc.scalar.activation(out=warm[:, 1:2], in_=warm[:, 0:1], func=EXP)
 
@@ -74,29 +74,33 @@ def tile_list_mlat_qf_exp_kernel(
         load_tab(1)
         for a, r in tab_rows[:6]:
             load_tab_scales(nc.sync, a, r)
-        for a, r in tab_rows[6:]:
-            load_tab_scales(nc.gpsimd, a, r)
+        for r in range(2):
+            nc.gpsimd.dma_start(out=wv4_s[r:P:32, :].bitcast(I32), in_=wv4_scales[0, r:16:4, :].bitcast(I32))
         ident = tile([P, P], F32, "ident")
         make_identity(nc, ident[:])
-        nc.sync.dma_start(out=wv8_raw[:], in_=wv8.rearrange("(p j) n -> p j n", j=PACK))
-        nc.sync.dma_start(out=wv4_w[:].bitcast(I32), in_=wv4_words[0].bitcast(I32))
-        for r in range(4):
-            nc.sync.dma_start(out=wv4_s[r:P:32, :].bitcast(I32), in_=wv4_scales[0, r:16:4, :].bitcast(I32))
+
+        def load_wv8(c):
+            cols = slice((N // 2) * c, (N // 2) * (c + 1))
+            nc.sync.dma_start(out=wv8_raw[c][:], in_=wv8.rearrange("(p j) n -> p j n", j=PACK)[:, :, cols])
+
         load_tab(0)
-        for a in range(2):
+        for a, r in tab_rows[6:]:
+            load_tab_scales(nc.sync, a, r)
+        nc.sync.dma_start(out=wv4_w[:].bitcast(I32), in_=wv4_words[0].bitcast(I32))
+        for r in range(2, 4):
+            nc.sync.dma_start(out=wv4_s[r:P:32, :].bitcast(I32), in_=wv4_scales[0, r:16:4, :].bitcast(I32))
+        load_wv8(0)
+        for g in range(2):
             nc.sync.dma_start(
-                out=x_raw[a][:], in_=x[512 * a : 512 * (a + 1), :].rearrange("(p j) m -> p j m", j=PACK)
+                out=x_raw[g][:], in_=x[512 * g : 512 * (g + 1), :].rearrange("(p j) m -> p j m", j=PACK)
             )
         for r in range(4):
             nc.sync.dma_start(
                 out=w8_s[W8_ROW + r : P : 32, :, :].bitcast(I32),
-                in_=w8_scales[:, r:16:4, :].rearrange("a q c -> q a c").bitcast(I32),
+                in_=w8_scales[:, r:16:4, :].rearrange("g q c -> q g c").bitcast(I32),
             )
-        for h in (1, 0):
-            nc.sync.dma_start(
-                out=w8_w[h][:],
-                in_=w8_words.rearrange("a p r i -> p a (r i)")[:, :, 4 * BANK * h : 4 * BANK * (h + 1)].bitcast(I32),
-            )
+        nc.sync.dma_start(out=w8_w[:], in_=w8_words.rearrange("g p r i -> p g (r i)").bitcast(I32))
+        load_wv8(1)
 
         def quantise(grouped, name, tag=""):
             width = grouped.shape[1]
@@ -113,33 +117,39 @@ def tile_list_mlat_qf_exp_kernel(
         got_s = {}
         got_w = {}
 
-        def gather_scales(h):
-            g = tile([P, BANK], U8, "got_s%d" % h)
+        def gather_scales(h, tag=""):
+            g = tile([P, BANK], U8, "got_s%d" % h, tag)
             nc.vector.tensor_copy(g[:], tab_s[:].indirect(listed(h)))
             got_s[h] = g
 
-        def gather_words(a, h):
-            g = tile([P, BANK], U32, "got_w%d%d" % (a, h))
+        def gather_words(a, h, tag=""):
+            g = tile([P, BANK], U32, "got_w%d%d" % (a, h), tag)
             nc.vector.tensor_copy(g[:], tab_w[a][:].bitcast(U32).indirect(listed(h)))
             got_w[(a, h)] = g
 
+        wv8_b = {}
         wv8_q = {}
 
-        def quantise_wv8(c):
-            grouped = tile([P, N // 2, PACK], BF16, "wv8_b%d" % c)
-            interleave(nc.scalar.copy, grouped[:], wv8_raw[:, :, (N // 2) * c : (N // 2) * (c + 1)])
-            wv8_q[c] = quantise(grouped, "wv8_q%d" % c, "tab_s" if c == 0 else "")
+        def interleave_wv8(engine_copy, nt):
+            wv8_b[nt] = tile([P, P, PACK], BF16, "wv8_b%d" % nt)
+            interleave(engine_copy, wv8_b[nt][:], wv8_raw[nt // 2][:, :, P * (nt % 2) : P * (nt % 2 + 1)])
+
+        def quantise_wv8(nt):
+            wv8_q[nt] = quantise(wv8_b[nt], "wv8_q%d" % nt)
+
+        def value_bank(nt, h):
+            return banks[4 * (nt // 2) + 2 * h + nt % 2]
 
         def value_pass(a, nt, h):
             if a == 1:
                 lhsT = wv4_w[:, 2 * P * nt : 2 * P * (nt + 1)].bitcast(FP4X4)
                 lhsT_scale = wv4_s[:, P * nt : P * (nt + 1)]
             else:
-                codes, scales = wv8_q[nt // 2]
-                lhsT = codes[:, P * (nt % 2) : P * (nt % 2 + 1)].bitcast(FP8X4)
-                lhsT_scale = scales[:, P * (nt % 2) : P * (nt % 2 + 1)]
+                codes, scales = wv8_q[nt]
+                lhsT = codes[:].bitcast(FP8X4)
+                lhsT_scale = scales[:]
             nc.tensor.matmul_mx(
-                out=banks[4 * h + nt][:],
+                out=value_bank(nt, h)[:],
                 lhsT=lhsT,
                 lhsT_scale=lhsT_scale,
                 rhs=got_w[(a, h)][:].bitcast(FP8X4),
@@ -147,6 +157,18 @@ def tile_list_mlat_qf_exp_kernel(
                 start=(a == 1),
                 stop=(a == 0),
             )
+
+        values = {}
+
+        def finish_values(engine_copy, nt, h, tag=""):
+            if h == 0:
+                values[nt] = tile([P, J], F32, "values%d" % nt, tag)
+            engine_copy(out=values[nt][:, BANK * h : BANK * (h + 1)], in_=value_bank(nt, h)[:])
+            if nt >= 2:
+                cols = slice(BANK * h, BANK * (h + 1))
+                nc.sync.dma_start(out=out_1[P * nt : P * (nt + 1), cols], in_=values[nt][:, cols])
+            elif h == 1:
+                nc.sync.dma_start(out=out_1[P * nt : P * (nt + 1), :], in_=values[nt][:])
 
         for h in range(2):
             gather_words(1, h)
@@ -160,80 +182,77 @@ def tile_list_mlat_qf_exp_kernel(
                 start=True,
                 stop=True,
             )
-        for h in range(2):
-            gather_scales(h)
-        for c in range(2):
-            quantise_wv8(c)
-        for h in range(2):
-            gather_words(0, h)
-        for a in (1, 0):
-            for h in range(2):
-                for nt in range(4):
-                    value_pass(a, nt, h)
+        gather_words(0, 0)
+        gather_scales(0)
+        for nt in range(2):
+            interleave_wv8(nc.scalar.copy, nt)
+        for nt in range(2):
+            quantise_wv8(nt)
+        gather_scales(1, "wv8_b0")
+        gather_words(0, 1, "wv8_b1")
+        for nt in range(2):
+            value_pass(1, nt, 0)
+        for nt in range(2):
+            value_pass(0, nt, 0)
+        for nt in range(2, 4):
+            value_pass(1, nt, 0)
+        for nt in range(4):
+            value_pass(1, nt, 1)
+        for nt in range(2):
+            value_pass(0, nt, 1)
 
         x_q = []
-        for a in range(2):
-            grouped = tile([P, M, PACK], BF16, "x_b%d" % a)
-            interleave(nc.scalar.copy, grouped[:], x_raw[a][:])
-            x_q.append(quantise(grouped, "x_q%d" % a))
+        for g in range(2):
+            grouped = tile([P, M, PACK], BF16, "x_b%d" % g)
+            interleave(nc.scalar.copy, grouped[:], x_raw[g][:])
+            x_q.append(quantise(grouped, "x_q%d" % g))
+            finish_values(nc.scalar.copy, g, 0, "x_raw%d" % g)
+        finish_values(nc.scalar.copy, 0, 1)
+        finish_values(nc.vector.tensor_copy, 1, 1)
 
-        values = tile([P, 4, J], F32, "values", "x_raw1")
-
-        def finish_values(nt):
-            nc.scalar.copy(out=values[:, nt, 0:BANK], in_=banks[nt][:])
-            nc.vector.tensor_copy(out=values[:, nt, BANK:J], in_=banks[4 + nt][:])
-            nc.sync.dma_start(out=out_1[P * nt : P * (nt + 1), :], in_=values[:, nt, :])
-
+        groups = [(a, mt) for mt in range(2) for a in (1, 0)]
+        for b, (a, mt) in enumerate(groups):
+            for g in range(2):
+                nc.tensor.matmul_mx(
+                    out=banks[b][:],
+                    lhsT=x_q[g][0][:, P * mt : P * (mt + 1)].bitcast(FP8X4),
+                    lhsT_scale=x_q[g][1][:, P * mt : P * (mt + 1)],
+                    rhs=w8_w[:, g, BANK * a : BANK * (a + 1)].bitcast(FP8X4),
+                    rhs_scale=w8_s[W8_ROW:P, g, BANK * a : BANK * (a + 1)],
+                    start=(g == 0),
+                    stop=(g == 1),
+                )
+        copy_on = {1: nc.scalar.copy, 0: nc.vector.tensor_copy}
         rows = {}
 
-        def project_queries(h, sum_banks):
-            for mt in range(2):
-                for a in range(2):
-                    nc.tensor.matmul_mx(
-                        out=sum_banks[mt][:],
-                        lhsT=x_q[a][0][:, P * mt : P * (mt + 1)].bitcast(FP8X4),
-                        lhsT_scale=x_q[a][1][:, P * mt : P * (mt + 1)],
-                        rhs=w8_w[h][:, a, :].bitcast(FP8X4),
-                        rhs_scale=w8_s[W8_ROW:P, a, BANK * h : BANK * (h + 1)],
-                        start=(a == 0),
-                        stop=(a == 1),
-                    )
+        def round_queries(mt):
+            for a in (1, 0):
+                row = tile([P, 2, P, 2], BF16, "qa_row%d%d" % (a, mt))
+                copy_on[max(a, 1 - mt)](out=row[:], in_=banks[2 * mt + 1 - a][:].rearrange("m (p u e) -> m u p e", u=2, e=2))
+                rows[(a, mt)] = row
 
-        def round_queries(h, sum_banks):
-            for mt, engine_copy in enumerate((nc.scalar.copy, nc.vector.tensor_copy)):
-                row = tile([P, 2, P, 2], BF16, "qa_row%d%d" % (h, mt))
-                engine_copy(out=row[:], in_=sum_banks[mt][:].rearrange("m (p u e) -> m u p e", u=2, e=2))
-                rows[(h, mt)] = row
+        qa_q = {}
 
-        def turn_half(h, mt, turn_bank):
-            words = rows[(h, mt)][:].rearrange("m u p e -> m (u p e)").bitcast(F32)
-            for u in range(2):
-                col = P * (2 * h + u)
-                nc.tensor.transpose(turn_bank[:, col : col + P], words[:, P * u : P * (u + 1)], ident[:])
-
-        def turn_queries(mt, turn_banks):
+        def turn_queries(mt):
             grouped = tile([P, 2 * P, PACK], BF16, "qa_b%d" % mt)
-            for h in (1, 0):
-                turn_half(h, mt, banks[turn_banks[h]])
-            if len(set(turn_banks)) == 1:
-                nc.scalar.copy(
-                    out=grouped[:].bitcast(F32).rearrange("p (h m) u -> p h m u", h=2),
-                    in_=banks[turn_banks[0]][:].rearrange("p (h u m) -> p h m u", h=2, u=2),
+            for a in (1, 0):
+                bank = banks[2 * mt + 1 - a]
+                words = rows[(a, mt)][:].rearrange("m u p e -> m (u p e)").bitcast(F32)
+                for u in range(2):
+                    nc.tensor.transpose(bank[:, P * u : P * (u + 1)], words[:, P * u : P * (u + 1)], ident[:])
+                copy_on[a](
+                    out=grouped[:, P * a : P * (a + 1), :].bitcast(F32),
+                    in_=bank[:, 0 : 2 * P].rearrange("p (u m) -> p m u", u=2),
                 )
-            else:
-                for h in (1, 0):
-                    nc.scalar.copy(
-                        out=grouped[:, P * h : P * (h + 1), :].bitcast(F32),
-                        in_=banks[turn_banks[h]][:, 2 * P * h : 2 * P * (h + 1)].rearrange("p (u m) -> p m u", u=2),
-                    )
-            return quantise(grouped, "qa_q%d" % mt)
+            qa_q[mt] = quantise(grouped, "qa_q%d" % mt)
 
-        def finish_scores(mt, qa_q, score_banks):
-            codes, scales = qa_q
+        def finish_scores(mt, stores):
+            codes, scales = qa_q[mt]
+            res = tile([P, J], F32, "exp%d" % mt)
             for h in range(2):
                 for a in range(2):
                     nc.tensor.matmul_mx(
-                        out=score_banks[h][:],
+                        out=banks[2 * mt + h][:],
                         lhsT=codes[:, P * a : P * (a + 1)].bitcast(FP8X4),
                         lhsT_scale=scales[:, P * a : P * (a + 1)],
                         rhs=got_w[(a, h)][:].bitcast(FP8X4),
@@ -241,22 +260,34 @@ def tile_list_mlat_qf_exp_kernel(
                         start=(a == 0),
                         stop=(a == 1),
                     )
-                res = tile([P, BANK], F32, "exp%d%d" % (mt, h))
-                nc.scalar.activation(out=res[:], in_=score_banks[h][:], func=EXP, scale=SCORE_SCALE)
-                nc.sync.dma_start(out=out_0[P * mt : P * (mt + 1), BANK * h : BANK * (h + 1)], in_=res[:])
+            done = 0
+            for lo, hi in stores:
+                for col in range(done, hi, BANK):
+                    end = min(col + BANK, hi)
+                    nc.scalar.activation(
+                        out=res[:, col:end],
+                        in_=banks[2 * mt + col // BANK][:, col % BANK : col % BANK + end - col],
+                        func=EXP,
+                        scale=SCORE_SCALE,
+                    )
+                done = hi
+                nc.sync.dma_start(out=out_0[P * mt : P * (mt + 1), lo:hi], in_=res[:, lo:hi])
 
-        finish_values(0)
-        finish_values(1)
-        project_queries(1, banks[0:2])
-        round_queries(1, banks[0:2])
-        project_queries(0, banks[4:6])
-        round_queries(0, banks[4:6])
-        finish_values(2)
-        nc.vector.tensor_copy(out=values[:, 3, 0:BANK], in_=banks[7][:])
-        nc.sync.dma_start(out=out_1[3 * P : 4 * P, BANK:J], in_=values[:, 3, 0:BANK])
-        qa_q = [turn_queries(0, (6, 2)), turn_queries(1, (7, 7))]
-        last = tile([P, BANK], F32, "last", "qa_row00")
-        nc.vector.tensor_copy(out=last[:], in_=banks[3][:])
-        nc.sync.dma_start(out=out_1[3 * P : 4 * P, 0:BANK], in_=last[:])
-        finish_scores(0, qa_q[0], banks[0:2])
-        finish_scores(1, qa_q[1], banks[4:6])
+        round_queries(0)
+        for nt in (2, 3):
+            interleave_wv8(nc.vector.tensor_copy, nt)
+        for nt in (2, 3):
+            quantise_wv8(nt)
+        round_queries(1)
+        value_pass(0, 2, 0)
+        finish_values(nc.scalar.copy, 2, 0)
+        turn_queries(0)
+        value_pass(0, 2, 1)
+        turn_queries(1)
+        for h in range(2):
+            value_pass(0, 3, h)
+        finish_values(nc.vector.tensor_copy, 2, 1)
+        finish_values(nc.scalar.copy, 3, 0)
+        finish_values(nc.vector.tensor_copy, 3, 1)
+        finish_scores(0, ((0, BANK), (BANK, J)))
+        finish_scores(1, ((0, BANK), (BANK, 3 * J // 4), (3 * J // 4, J)))

@@ -290,4 +290,4 @@ def tile_list_mlat_qf_exp_kernel(
         finish_values(nc.scalar.copy, 3, 0)
         finish_values(nc.vector.tensor_copy, 3, 1)
         finish_scores(0, ((0, BANK), (BANK, J)))
-        finish_scores(1, ((0, BANK), (BANK, 3 * J // 4), (3 * J // 4, J)))
+        finish_scores(1, ((0, BANK), (BANK, J)))

@@ -130,8 +130,8 @@ def tile_list_mlat_qf_exp_kernel(
         wv8_b = {}
         wv8_q = {}
 
-        def interleave_wv8(engine_copy, nt):
-            wv8_b[nt] = tile([P, P, PACK], BF16, "wv8_b%d" % nt)
+        def interleave_wv8(engine_copy, nt, tag=""):
+            wv8_b[nt] = tile([P, P, PACK], BF16, "wv8_b%d" % nt, tag)
             interleave(engine_copy, wv8_b[nt][:], wv8_raw[nt // 2][:, :, P * (nt % 2) : P * (nt % 2 + 1)])
 
         def quantise_wv8(nt):
@@ -275,8 +275,7 @@ def tile_list_mlat_qf_exp_kernel(
 
         round_queries(0)
         for nt in (2, 3):
-            interleave_wv8(nc.vector.tensor_copy, nt)
-        for nt in (2, 3):
+            interleave_wv8(nc.vector.tensor_copy, nt, "wv8_b2")
             quantise_wv8(nt)
         round_queries(1)
         value_pass(0, 2, 0)

@@ -51,7 +51,8 @@ def tile_list_mlat_qf_exp_kernel(
         x_raw = [tile([P, PACK, M], F32, "x_raw%d" % a) for a in range(2)]
         w8_w = tile([P, 2, R], I32, "w8_w")
         tab_w = [tile([P, T], I32, "tab_w%d" % a) for a in range(2)]
-        wv8_raw = [tile([P, PACK, N // 2], F32, "wv8_raw%d" % c) for c in range(2)]
+        wv8_cols = ((0, 2 * P), (2 * P, 3 * P), (3 * P, N))
+        wv8_raw = [tile([P, PACK, hi - lo], F32, "wv8_raw%d" % lo) for lo, hi in wv8_cols]
         wv4_w = tile([P, 2 * N], U8, "wv4_w")
 
         nc.gpsimd.memset(tab_s[:].bitcast(I32), 0)
@@ -76,11 +77,16 @@ def tile_list_mlat_qf_exp_kernel(
             load_tab_scales(nc.sync, a, r)
         for r in range(2):
             nc.gpsimd.dma_start(out=wv4_s[r:P:32, :].bitcast(I32), in_=wv4_scales[0, r:16:4, :].bitcast(I32))
+        for r in range(4):
+            nc.gpsimd.dma_start(
+                out=w8_s[W8_ROW + r : P : 32, :, :].bitcast(I32),
+                in_=w8_scales[:, r:16:4, :].rearrange("g q c -> q g c").bitcast(I32),
+            )
         ident = tile([P, P], F32, "ident")
         make_identity(nc, ident[:])
 
         def load_wv8(c):
-            cols = slice((N // 2) * c, (N // 2) * (c + 1))
+            cols = slice(*wv8_cols[c])
             nc.sync.dma_start(out=wv8_raw[c][:], in_=wv8.rearrange("(p j) n -> p j n", j=PACK)[:, :, cols])
 
         load_tab(0)
@@ -90,17 +96,13 @@ def tile_list_mlat_qf_exp_kernel(
         for r in range(2, 4):
             nc.sync.dma_start(out=wv4_s[r:P:32, :].bitcast(I32), in_=wv4_scales[0, r:16:4, :].bitcast(I32))
         load_wv8(0)
+        load_wv8(1)
         for g in range(2):
             nc.sync.dma_start(
                 out=x_raw[g][:], in_=x[512 * g : 512 * (g + 1), :].rearrange("(p j) m -> p j m", j=PACK)
             )
-        for r in range(4):
-            nc.sync.dma_start(
-                out=w8_s[W8_ROW + r : P : 32, :, :].bitcast(I32),
-                in_=w8_scales[:, r:16:4, :].rearrange("g q c -> q g c").bitcast(I32),
-            )
         nc.sync.dma_start(out=w8_w[:], in_=w8_words.rearrange("g p r i -> p g (r i)").bitcast(I32))
-        load_wv8(1)
+        load_wv8(2)
 
         def quantise(grouped, name, tag=""):
             width = grouped.shape[1]
@@ -111,8 +113,8 @@ def tile_list_mlat_qf_exp_kernel(
             )
             return codes, scales
 
-        def listed(h):
-            return offsets[:, (BANK // 16) * h : (BANK // 16) * (h + 1)]
+        def listed(h, lo=0, hi=BANK):
+            return offsets[:, (BANK * h + lo) // 16 : (BANK * h + hi) // 16]
 
         got_s = {}
         got_w = {}
@@ -122,17 +124,30 @@ def tile_list_mlat_qf_exp_kernel(
             nc.vector.tensor_copy(g[:], tab_s[:].indirect(listed(h)))
             got_s[h] = g
 
-        def gather_words(a, h, tag=""):
-            g = tile([P, BANK], U32, "got_w%d%d" % (a, h), tag)
-            nc.vector.tensor_copy(g[:], tab_w[a][:].bitcast(U32).indirect(listed(h)))
-            got_w[(a, h)] = g
+        def gather_words(a, h, tag="", lo=0, hi=BANK):
+            g = tile([P, hi - lo], U32, "got_w%d%d_%d" % (a, h, lo), tag)
+            nc.vector.tensor_copy(g[:], tab_w[a][:].bitcast(U32).indirect(listed(h, lo, hi)))
+            got_w.setdefault((a, h), []).append((lo, hi, g))
+
+        def table_pass(bank, lhsT, lhsT_scale, a, h, start, stop):
+            pieces = got_w[(a, h)]
+            for i, (lo, hi, g) in enumerate(pieces):
+                nc.tensor.matmul_mx(
+                    out=bank[:, lo:hi],
+                    lhsT=lhsT,
+                    lhsT_scale=lhsT_scale,
+                    rhs=g[:].bitcast(FP8X4),
+                    rhs_scale=got_s[h][TAB_ROW[a] : P, lo:hi],
+                    start=start and i == 0,
+                    stop=stop and i == len(pieces) - 1,
+                )
 
         wv8_b = {}
         wv8_q = {}
 
         def interleave_wv8(engine_copy, nt, tag=""):
             wv8_b[nt] = tile([P, P, PACK], BF16, "wv8_b%d" % nt, tag)
-            interleave(engine_copy, wv8_b[nt][:], wv8_raw[nt // 2][:, :, P * (nt % 2) : P * (nt % 2 + 1)])
+            interleave(engine_copy, wv8_b[nt][:], wv8_raw[max(nt - 1, 0)][:, :, P * (nt == 1) : P * (nt == 1) + P])
 
         def quantise_wv8(nt):
             wv8_q[nt] = quantise(wv8_b[nt], "wv8_q%d" % nt)
@@ -148,15 +163,7 @@ def tile_list_mlat_qf_exp_kernel(
                 codes, scales = wv8_q[nt]
                 lhsT = codes[:].bitcast(FP8X4)
                 lhsT_scale = scales[:]
-            nc.tensor.matmul_mx(
-                out=value_bank(nt, h)[:],
-                lhsT=lhsT,
-                lhsT_scale=lhsT_scale,
-                rhs=got_w[(a, h)][:].bitcast(FP8X4),
-                rhs_scale=got_s[h][TAB_ROW[a] : P, :],
-                start=(a == 1),
-                stop=(a == 0),
-            )
+            table_pass(value_bank(nt, h), lhsT, lhsT_scale, a, h, a == 1, a == 0)
 
         values = {}
 
@@ -172,33 +179,33 @@ def tile_list_mlat_qf_exp_kernel(
 
         for h in range(2):
             gather_words(1, h)
-        for nt in range(3):
+        for nt in range(2):
             nc.tensor.matmul_mx(
                 out=banks[7][:],
                 lhsT=wv4_w[:, 2 * P * nt : 2 * P * (nt + 1)].bitcast(FP4X4),
                 lhsT_scale=wv4_s[:, P * nt : P * (nt + 1)],
-                rhs=got_w[(1, 0)][:].bitcast(FP8X4),
+                rhs=got_w[(1, 0)][0][2][:].bitcast(FP8X4),
                 rhs_scale=wv4_s[:],
                 start=True,
                 stop=True,
             )
-        gather_words(0, 0)
-        gather_scales(0)
-        for nt in range(2):
+        gather_words(0, 0, "", 0, BANK // 2)
+        for h in range(2):
+            gather_scales(h)
+        gather_words(0, 0, "tab_s", BANK // 2, BANK)
+        for nt in range(3):
             interleave_wv8(nc.scalar.copy, nt)
         for nt in range(2):
             quantise_wv8(nt)
-        gather_scales(1, "wv8_b0")
-        gather_words(0, 1, "wv8_b1")
-        for nt in range(2):
-            value_pass(1, nt, 0)
+        quantise_wv8(2)
+        gather_words(0, 1, "wv8_b2")
+        for h in range(2):
+            for nt in range(4):
+                value_pass(1, nt, h)
         for nt in range(2):
             value_pass(0, nt, 0)
-        for nt in range(2, 4):
-            value_pass(1, nt, 0)
-        for nt in range(4):
-            value_pass(1, nt, 1)
-        for nt in range(2):
+        value_pass(0, 2, 0)
+        for nt in range(3):
             value_pass(0, nt, 1)
 
         x_q = []
@@ -209,6 +216,8 @@ def tile_list_mlat_qf_exp_kernel(
             finish_values(nc.scalar.copy, g, 0, "x_raw%d" % g)
         finish_values(nc.scalar.copy, 0, 1)
         finish_values(nc.vector.tensor_copy, 1, 1)
+        finish_values(nc.vector.tensor_copy, 2, 0, "x_b1")
+        finish_values(nc.vector.tensor_copy, 2, 1)
 
         groups = [(a, mt) for mt in range(2) for a in (1, 0)]
         for b, (a, mt) in enumerate(groups):
@@ -250,16 +259,9 @@ def tile_list_mlat_qf_exp_kernel(
             codes, scales = qa_q[mt]
             res = tile([P, J], F32, "exp%d" % mt)
             for h in range(2):
-                for a in range(2):
-                    nc.tensor.matmul_mx(
-                        out=banks[2 * mt + h][:],
-                        lhsT=codes[:, P * a : P * (a + 1)].bitcast(FP8X4),
-                        lhsT_scale=scales[:, P * a : P * (a + 1)],
-                        rhs=got_w[(a, h)][:].bitcast(FP8X4),
-                        rhs_scale=got_s[h][TAB_ROW[a] : P, :],
-                        start=(a == 0),
-                        stop=(a == 1),
-                    )
+                for a in (1, 0):
+                    cols = slice(P * a, P * (a + 1))
+                    table_pass(banks[2 * mt + h], codes[:, cols].bitcast(FP8X4), scales[:, cols], a, h, a == 1, a == 0)
             done = 0
             for lo, hi in stores:
                 for col in range(done, hi, BANK):
@@ -274,19 +276,14 @@ def tile_list_mlat_qf_exp_kernel(
                 nc.sync.dma_start(out=out_0[P * mt : P * (mt + 1), lo:hi], in_=res[:, lo:hi])
 
         round_queries(0)
-        for nt in (2, 3):
-            interleave_wv8(nc.vector.tensor_copy, nt, "wv8_b2")
-            quantise_wv8(nt)
+        interleave_wv8(nc.vector.tensor_copy, 3)
+        quantise_wv8(3)
         round_queries(1)
-        value_pass(0, 2, 0)
-        finish_values(nc.scalar.copy, 2, 0)
         turn_queries(0)
-        value_pass(0, 2, 1)
-        turn_queries(1)
-        for h in range(2):
-            value_pass(0, 3, h)
-        finish_values(nc.vector.tensor_copy, 2, 1)
+        value_pass(0, 3, 0)
         finish_values(nc.scalar.copy, 3, 0)
+        turn_queries(1)
+        value_pass(0, 3, 1)
         finish_values(nc.vector.tensor_copy, 3, 1)
         finish_scores(0, ((0, BANK), (BANK, J)))
         finish_scores(1, ((0, BANK), (BANK, J)))

@@ -15,6 +15,8 @@ U8 = mybir.dt.uint8
 FP8X4 = mybir.dt.float8_e4m3fn_x4
 FP4X4 = mybir.dt.float4_e2m1fn_x4
 EXP = mybir.ActivationFunctionType.Exp
+MULT = mybir.AluOpType.mult
+ADD = mybir.AluOpType.add
 
 P = 128
 PACK = 4
@@ -127,7 +129,7 @@ def tile_list_mlat_qf_exp_kernel(
         def gather_words(a, h, tag="", lo=0, hi=BANK):
             g = tile([P, hi - lo], U32, "got_w%d%d_%d" % (a, h, lo), tag)
             nc.vector.tensor_copy(g[:], tab_w[a][:].bitcast(U32).indirect(listed(h, lo, hi)))
-            got_w.setdefault((a, h), []).append((lo, hi, g))
+            got_w.setdefault((a, h), []).append((lo, hi, g[:]))
 
         def table_pass(bank, lhsT, lhsT_scale, a, h, start, stop):
             pieces = got_w[(a, h)]
@@ -136,11 +138,14 @@ def tile_list_mlat_qf_exp_kernel(
                     out=bank[:, lo:hi],
                     lhsT=lhsT,
                     lhsT_scale=lhsT_scale,
-                    rhs=g[:].bitcast(FP8X4),
+                    rhs=g.bitcast(FP8X4),
                     rhs_scale=got_s[h][TAB_ROW[a] : P, lo:hi],
                     start=start and i == 0,
                     stop=stop and i == len(pieces) - 1,
                 )
+
+        def pool_copy(out, in_):
+            nc.gpsimd.tensor_scalar(out=out, in0=in_, scalar1=1.0, scalar2=0.0, op0=MULT, op1=ADD)
 
         wv8_b = {}
         wv8_q = {}
@@ -150,7 +155,8 @@ def tile_list_mlat_qf_exp_kernel(
             interleave(engine_copy, wv8_b[nt][:], wv8_raw[max(nt - 1, 0)][:, :, P * (nt == 1) : P * (nt == 1) + P])
 
         def quantise_wv8(nt):
-            wv8_q[nt] = quantise(wv8_b[nt], "wv8_q%d" % nt)
+            codes, scales = quantise(wv8_b[nt], "wv8_q%d" % nt)
+            wv8_q[nt] = (codes[:], scales[:])
 
         def value_bank(nt, h):
             return banks[4 * (nt // 2) + 2 * h + nt % 2]
@@ -161,8 +167,8 @@ def tile_list_mlat_qf_exp_kernel(
                 lhsT_scale = wv4_s[:, P * nt : P * (nt + 1)]
             else:
                 codes, scales = wv8_q[nt]
-                lhsT = codes[:].bitcast(FP8X4)
-                lhsT_scale = scales[:]
+                lhsT = codes.bitcast(FP8X4)
+                lhsT_scale = scales
             table_pass(value_bank(nt, h), lhsT, lhsT_scale, a, h, a == 1, a == 0)
 
         values = {}
@@ -177,14 +183,16 @@ def tile_list_mlat_qf_exp_kernel(
             elif h == 1:
                 nc.sync.dma_start(out=out_1[P * nt : P * (nt + 1), :], in_=values[nt][:])
 
+        got_w1 = tile([P, J], U32, "got_w1")
+        nc.vector.tensor_copy(got_w1[:], tab_w[1][:].bitcast(U32).indirect(offsets[:]))
         for h in range(2):
-            gather_words(1, h)
+            got_w[(1, h)] = [(0, BANK, got_w1[:, BANK * h : BANK * (h + 1)])]
         for nt in range(2):
             nc.tensor.matmul_mx(
                 out=banks[7][:],
                 lhsT=wv4_w[:, 2 * P * nt : 2 * P * (nt + 1)].bitcast(FP4X4),
                 lhsT_scale=wv4_s[:, P * nt : P * (nt + 1)],
-                rhs=got_w[(1, 0)][0][2][:].bitcast(FP8X4),
+                rhs=got_w[(1, 0)][0][2].bitcast(FP8X4),
                 rhs_scale=wv4_s[:],
                 start=True,
                 stop=True,
@@ -193,10 +201,12 @@ def tile_list_mlat_qf_exp_kernel(
         for h in range(2):
             gather_scales(h)
         gather_words(0, 0, "tab_s", BANK // 2, BANK)
-        for nt in range(3):
-            interleave_wv8(nc.scalar.copy, nt)
+        lower_b = tile([P, 2 * P, PACK], BF16, "lower_b")
+        interleave(nc.scalar.copy, lower_b[:], wv8_raw[0][:])
+        interleave_wv8(pool_copy, 2)
+        codes, scales = quantise(lower_b, "lower_q")
         for nt in range(2):
-            quantise_wv8(nt)
+            wv8_q[nt] = (codes[:, P * nt : P * (nt + 1)], scales[:, P * nt : P * (nt + 1)])
         quantise_wv8(2)
         gather_words(0, 1, "wv8_b2")
         for h in range(2):

@@ -177,11 +177,8 @@ def tile_list_mlat_qf_exp_kernel(
             if h == 0:
                 values[nt] = tile([P, J], F32, "values%d" % nt, tag)
             engine_copy(out=values[nt][:, BANK * h : BANK * (h + 1)], in_=value_bank(nt, h)[:])
-            if nt >= 2:
-                cols = slice(BANK * h, BANK * (h + 1))
-                nc.sync.dma_start(out=out_1[P * nt : P * (nt + 1), cols], in_=values[nt][:, cols])
-            elif h == 1:
-                nc.sync.dma_start(out=out_1[P * nt : P * (nt + 1), :], in_=values[nt][:])
+            cols = slice(BANK * h, BANK * (h + 1))
+            nc.sync.dma_start(out=out_1[P * nt : P * (nt + 1), cols], in_=values[nt][:, cols])
 
         got_w1 = tile([P, J], U32, "got_w1")
         nc.vector.tensor_copy(got_w1[:], tab_w[1][:].bitcast(U32).indirect(offsets[:]))

@@ -42,7 +42,7 @@ def tile_list_mlat_qf_exp_kernel(
         psum = ctx.enter_context(tc.psum_pool(name="psum", bufs=1))
 
         def tile(shape, dtype, name, tag=""):
-            return sb.tile(shape, dtype, name=name, tag=tag or name, align_bytes=64)
+            return sb.tile(shape, dtype, name=name, tag=tag or name, align_bytes=256)
 
         banks = [psum.tile([P, BANK], F32, name="bank%d" % b) for b in range(8)]
         offsets = sb.tile([P, J // 16], U16, name="offsets")

@@ -205,15 +205,29 @@ def tile_list_mlat_qf_exp_kernel(
         for nt in range(2):
             wv8_q[nt] = (codes[:, P * nt : P * (nt + 1)], scales[:, P * nt : P * (nt + 1)])
         quantise_wv8(2)
-        gather_words(0, 1, "wv8_b2")
+        got_last = tile([P, BANK], U32, "got_w01", "wv8_b2")
+        quarters = ((0, BANK // 2), (BANK // 2, BANK))
+        for lo, hi in quarters:
+            nc.vector.tensor_copy(got_last[:, lo:hi], tab_w[0][:].bitcast(U32).indirect(listed(1, lo, hi)))
+        got_w[(0, 1)] = [(0, BANK, got_last[:])]
         for h in range(2):
             for nt in range(4):
                 value_pass(1, nt, h)
         for nt in range(2):
             value_pass(0, nt, 0)
         value_pass(0, 2, 0)
-        for nt in range(3):
-            value_pass(0, nt, 1)
+        for lo, hi in quarters:
+            for nt in range(3):
+                codes, scales = wv8_q[nt]
+                nc.tensor.matmul_mx(
+                    out=value_bank(nt, 1)[:, lo:hi],
+                    lhsT=codes.bitcast(FP8X4),
+                    lhsT_scale=scales,
+                    rhs=got_last[:, lo:hi].bitcast(FP8X4),
+                    rhs_scale=got_s[1][TAB_ROW[0] : P, lo:hi],
+                    start=False,
+                    stop=(hi == BANK),
+                )
 
         x_q = []
         for g in range(2):

from contextlib import ExitStack

import concourse.mybir as mybir
from concourse.masks import make_identity

K, R, M, T, N, J = 1024, 1024, 256, 2048, 512, 1024
FLOPS = 2 * K * R * M + 2 * R * M * J + 2 * R * N * J

F32 = mybir.dt.float32
BF16 = mybir.dt.bfloat16
I32 = mybir.dt.int32
U32 = mybir.dt.uint32
U16 = mybir.dt.uint16
U8 = mybir.dt.uint8
FP8X4 = mybir.dt.float8_e4m3fn_x4
FP4X4 = mybir.dt.float4_e2m1fn_x4
EXP = mybir.ActivationFunctionType.Exp
MULT = mybir.AluOpType.mult
ADD = mybir.AluOpType.add

P = 128
PACK = 4
BANK = 512
TAB_ROW = (4, 0)
W8_ROW = 8
SCORE_SCALE = 0.015625


def interleave(engine_copy, grouped, raw):
    engine_copy(
        out=grouped.rearrange("p (c i) t -> p c t i", i=4),
        in_=raw.rearrange("p t (c i) -> p c t i", i=4),
    )


def tile_list_mlat_qf_exp_kernel(
    tc, x, w8_words, w8_scales, tab_words, tab_scales, wv8, wv4_words, wv4_scales, offs, out_0, out_1
):
    nc = tc.nc
    with ExitStack() as ctx:
        sb = ctx.enter_context(tc.tile_pool(name="sb", bufs=1))
        psum = ctx.enter_context(tc.psum_pool(name="psum", bufs=1))

        def tile(shape, dtype, name, tag=""):
            return sb.tile(shape, dtype, name=name, tag=tag or name, align_bytes=256)

        banks = [psum.tile([P, BANK], F32, name="bank%d" % b) for b in range(8)]
        offsets = sb.tile([P, J // 16], U16, name="offsets")
        tab_s = tile([P, T], U8, "tab_s")
        w8_s = tile([P, 2, R], U8, "w8_s")
        wv4_s = tile([P, N], U8, "wv4_s")
        warm = tile([P, 2], F32, "warm")
        x_raw = [tile([P, PACK, M], F32, "x_raw%d" % a) for a in range(2)]
        w8_w = tile([P, 2, R], I32, "w8_w")
        tab_w = [tile([P, T], I32, "tab_w%d" % a) for a in range(2)]
        wv8_cols = ((0, 2 * P), (2 * P, 3 * P), (3 * P, N))
        wv8_raw = [tile([P, PACK, hi - lo], F32, "wv8_raw%d" % lo) for lo, hi in wv8_cols]
        wv4_w = tile([P, 2 * N], U8, "wv4_w")

        nc.gpsimd.memset(tab_s[:].bitcast(I32), 0)
        nc.gpsimd.memset(wv4_s[:].bitcast(I32), 0)
        nc.vector.memset(warm[:, 0:1], 0.0)
        nc.vector.memset(w8_s[:].bitcast(I32), 0)
        nc.scalar.activation(out=warm[:, 1:2], in_=warm[:, 0:1], func=EXP)

        def load_tab_scales(queue, a, r):
            queue.dma_start(
                out=tab_s[TAB_ROW[a] + r : P : 32, :].bitcast(I32),
                in_=tab_scales[a, r:16:4, :].bitcast(I32),
            )

        def load_tab(a):
            nc.sync.dma_start(out=tab_w[a][:], in_=tab_words[a].rearrange("p t i -> p (t i)").bitcast(I32))

        tab_rows = [(a, r) for r in range(4) for a in range(2)]
        nc.sync.dma_start(offsets[:], offs)
        load_tab(1)
        for a, r in tab_rows[:6]:
            load_tab_scales(nc.sync, a, r)
        for r in range(2):
            nc.gpsimd.dma_start(out=wv4_s[r:P:32, :].bitcast(I32), in_=wv4_scales[0, r:16:4, :].bitcast(I32))
        for r in range(4):
            nc.gpsimd.dma_start(
                out=w8_s[W8_ROW + r : P : 32, :, :].bitcast(I32),
                in_=w8_scales[:, r:16:4, :].rearrange("g q c -> q g c").bitcast(I32),
            )
        ident = tile([P, P], F32, "ident")
        make_identity(nc, ident[:])

        def load_wv8(c):
            cols = slice(*wv8_cols[c])
            nc.sync.dma_start(out=wv8_raw[c][:], in_=wv8.rearrange("(p j) n -> p j n", j=PACK)[:, :, cols])

        load_tab(0)
        for a, r in tab_rows[6:]:
            load_tab_scales(nc.sync, a, r)
        nc.sync.dma_start(out=wv4_w[:].bitcast(I32), in_=wv4_words[0].bitcast(I32))
        for r in range(2, 4):
            nc.sync.dma_start(out=wv4_s[r:P:32, :].bitcast(I32), in_=wv4_scales[0, r:16:4, :].bitcast(I32))
        load_wv8(0)
        load_wv8(1)
        for g in range(2):
            nc.sync.dma_start(
                out=x_raw[g][:], in_=x[512 * g : 512 * (g + 1), :].rearrange("(p j) m -> p j m", j=PACK)
            )
        nc.sync.dma_start(out=w8_w[:], in_=w8_words.rearrange("g p r i -> p g (r i)").bitcast(I32))
        load_wv8(2)

        def quantise(grouped, name, tag=""):
            width = grouped.shape[1]
            codes = tile([P, width], U32, name + "_w", tag)
            scales = tile([P, width], U8, name + "_s")
            nc.vector.quantize_mx(
                out=codes[:].bitcast(FP8X4), scales=scales[:], in_=grouped[:].rearrange("p w t -> p (w t)")
            )
            return codes, scales

        def listed(h, lo=0, hi=BANK):
            return offsets[:, (BANK * h + lo) // 16 : (BANK * h + hi) // 16]

        got_s = {}
        got_w = {}

        def gather_scales(h, tag=""):
            g = tile([P, BANK], U8, "got_s%d" % h, tag)
            nc.vector.tensor_copy(g[:], tab_s[:].indirect(listed(h)))
            got_s[h] = g

        def gather_words(a, h, tag="", lo=0, hi=BANK):
            g = tile([P, hi - lo], U32, "got_w%d%d_%d" % (a, h, lo), tag)
            nc.vector.tensor_copy(g[:], tab_w[a][:].bitcast(U32).indirect(listed(h, lo, hi)))
            got_w.setdefault((a, h), []).append((lo, hi, g[:]))

        def table_pass(bank, lhsT, lhsT_scale, a, h, start, stop):
            pieces = got_w[(a, h)]
            for i, (lo, hi, g) in enumerate(pieces):
                nc.tensor.matmul_mx(
                    out=bank[:, lo:hi],
                    lhsT=lhsT,
                    lhsT_scale=lhsT_scale,
                    rhs=g.bitcast(FP8X4),
                    rhs_scale=got_s[h][TAB_ROW[a] : P, lo:hi],
                    start=start and i == 0,
                    stop=stop and i == len(pieces) - 1,
                )

        def pool_copy(out, in_):
            nc.gpsimd.tensor_scalar(out=out, in0=in_, scalar1=1.0, scalar2=0.0, op0=MULT, op1=ADD)

        wv8_b = {}
        wv8_q = {}

        def interleave_wv8(engine_copy, nt, tag=""):
            wv8_b[nt] = tile([P, P, PACK], BF16, "wv8_b%d" % nt, tag)
            interleave(engine_copy, wv8_b[nt][:], wv8_raw[max(nt - 1, 0)][:, :, P * (nt == 1) : P * (nt == 1) + P])

        def quantise_wv8(nt):
            codes, scales = quantise(wv8_b[nt], "wv8_q%d" % nt)
            wv8_q[nt] = (codes[:], scales[:])

        def value_bank(nt, h):
            return banks[4 * (nt // 2) + 2 * h + nt % 2]

        def value_pass(a, nt, h):
            if a == 1:
                lhsT = wv4_w[:, 2 * P * nt : 2 * P * (nt + 1)].bitcast(FP4X4)
                lhsT_scale = wv4_s[:, P * nt : P * (nt + 1)]
            else:
                codes, scales = wv8_q[nt]
                lhsT = codes.bitcast(FP8X4)
                lhsT_scale = scales
            table_pass(value_bank(nt, h), lhsT, lhsT_scale, a, h, a == 1, a == 0)

        values = {}

        def finish_values(engine_copy, nt, h, tag=""):
            if h == 0:
                values[nt] = tile([P, J], F32, "values%d" % nt, tag)
            engine_copy(out=values[nt][:, BANK * h : BANK * (h + 1)], in_=value_bank(nt, h)[:])
            cols = slice(BANK * h, BANK * (h + 1))
            nc.sync.dma_start(out=out_1[P * nt : P * (nt + 1), cols], in_=values[nt][:, cols])

        got_w1 = tile([P, J], U32, "got_w1")
        nc.vector.tensor_copy(got_w1[:], tab_w[1][:].bitcast(U32).indirect(offsets[:]))
        for h in range(2):
            got_w[(1, h)] = [(0, BANK, got_w1[:, BANK * h : BANK * (h + 1)])]
        for nt in range(2):
            nc.tensor.matmul_mx(
                out=banks[7][:],
                lhsT=wv4_w[:, 2 * P * nt : 2 * P * (nt + 1)].bitcast(FP4X4),
                lhsT_scale=wv4_s[:, P * nt : P * (nt + 1)],
                rhs=got_w[(1, 0)][0][2].bitcast(FP8X4),
                rhs_scale=wv4_s[:],
                start=True,
                stop=True,
            )
        gather_words(0, 0, "", 0, BANK // 2)
        for h in range(2):
            gather_scales(h)
        gather_words(0, 0, "tab_s", BANK // 2, BANK)
        lower_b = tile([P, 2 * P, PACK], BF16, "lower_b")
        interleave(nc.scalar.copy, lower_b[:], wv8_raw[0][:])
        interleave_wv8(pool_copy, 2)
        codes, scales = quantise(lower_b, "lower_q")
        for nt in range(2):
            wv8_q[nt] = (codes[:, P * nt : P * (nt + 1)], scales[:, P * nt : P * (nt + 1)])
        quantise_wv8(2)
        got_last = tile([P, BANK], U32, "got_w01", "wv8_b2")
        quarters = ((0, BANK // 2), (BANK // 2, BANK))
        for lo, hi in quarters:
            nc.vector.tensor_copy(got_last[:, lo:hi], tab_w[0][:].bitcast(U32).indirect(listed(1, lo, hi)))
        got_w[(0, 1)] = [(0, BANK, got_last[:])]
        for h in range(2):
            for nt in range(4):
                value_pass(1, nt, h)
        for nt in range(2):
            value_pass(0, nt, 0)
        value_pass(0, 2, 0)
        for lo, hi in quarters:
            for nt in range(3):
                codes, scales = wv8_q[nt]
                nc.tensor.matmul_mx(
                    out=value_bank(nt, 1)[:, lo:hi],
                    lhsT=codes.bitcast(FP8X4),
                    lhsT_scale=scales,
                    rhs=got_last[:, lo:hi].bitcast(FP8X4),
                    rhs_scale=got_s[1][TAB_ROW[0] : P, lo:hi],
                    start=False,
                    stop=(hi == BANK),
                )

        x_q = []
        for g in range(2):
            grouped = tile([P, M, PACK], BF16, "x_b%d" % g)
            interleave(nc.scalar.copy, grouped[:], x_raw[g][:])
            x_q.append(quantise(grouped, "x_q%d" % g))
            finish_values(nc.scalar.copy, g, 0, "x_raw%d" % g)
        finish_values(nc.scalar.copy, 0, 1)
        finish_values(nc.vector.tensor_copy, 1, 1)
        finish_values(nc.vector.tensor_copy, 2, 0, "x_b1")
        finish_values(nc.vector.tensor_copy, 2, 1)

        groups = [(a, mt) for mt in range(2) for a in (1, 0)]
        for b, (a, mt) in enumerate(groups):
            for g in range(2):
                nc.tensor.matmul_mx(
                    out=banks[b][:],
                    lhsT=x_q[g][0][:, P * mt : P * (mt + 1)].bitcast(FP8X4),
                    lhsT_scale=x_q[g][1][:, P * mt : P * (mt + 1)],
                    rhs=w8_w[:, g, BANK * a : BANK * (a + 1)].bitcast(FP8X4),
                    rhs_scale=w8_s[W8_ROW:P, g, BANK * a : BANK * (a + 1)],
                    start=(g == 0),
                    stop=(g == 1),
                )
        copy_on = {1: nc.scalar.copy, 0: nc.vector.tensor_copy}
        rows = {}

        def round_queries(mt):
            for a in (1, 0):
                row = tile([P, 2, P, 2], BF16, "qa_row%d%d" % (a, mt))
                copy_on[max(a, 1 - mt)](out=row[:], in_=banks[2 * mt + 1 - a][:].rearrange("m (p u e) -> m u p e", u=2, e=2))
                rows[(a, mt)] = row

        qa_q = {}

        def turn_queries(mt):
            grouped = tile([P, 2 * P, PACK], BF16, "qa_b%d" % mt)
            for a in (1, 0):
                bank = banks[2 * mt + 1 - a]
                words = rows[(a, mt)][:].rearrange("m u p e -> m (u p e)").bitcast(F32)
                for u in range(2):
                    nc.tensor.transpose(bank[:, P * u : P * (u + 1)], words[:, P * u : P * (u + 1)], ident[:])
                copy_on[a](
                    out=grouped[:, P * a : P * (a + 1), :].bitcast(F32),
                    in_=bank[:, 0 : 2 * P].rearrange("p (u m) -> p m u", u=2),
                )
            qa_q[mt] = quantise(grouped, "qa_q%d" % mt)

        def finish_scores(mt, stores):
            codes, scales = qa_q[mt]
            res = tile([P, J], F32, "exp%d" % mt)
            for h in range(2):
                for a in (1, 0):
                    cols = slice(P * a, P * (a + 1))
                    table_pass(banks[2 * mt + h], codes[:, cols].bitcast(FP8X4), scales[:, cols], a, h, a == 1, a == 0)
            done = 0
            for lo, hi in stores:
                for col in range(done, hi, BANK):
                    end = min(col + BANK, hi)
                    nc.scalar.activation(
                        out=res[:, col:end],
                        in_=banks[2 * mt + col // BANK][:, col % BANK : col % BANK + end - col],
                        func=EXP,
                        scale=SCORE_SCALE,
                    )
                done = hi
                nc.sync.dma_start(out=out_0[P * mt : P * (mt + 1), lo:hi], in_=res[:, lo:hi])

        round_queries(0)
        interleave_wv8(nc.vector.tensor_copy, 3)
        quantise_wv8(3)
        round_queries(1)
        turn_queries(0)
        value_pass(0, 3, 0)
        finish_values(nc.scalar.copy, 3, 0)
        turn_queries(1)
        value_pass(0, 3, 1)
        finish_values(nc.vector.tensor_copy, 3, 1)
        finish_scores(0, ((0, BANK), (BANK, J)))
        finish_scores(1, ((0, BANK), (BANK, J)))
